import numpy as np
import ml_dtypes


def mxq(x, axis, fmt="e4m3"):
    dtype, down = {"e4m3": (ml_dtypes.float8_e4m3fn, 7), "e5m2": (ml_dtypes.float8_e5m2, 14)}[fmt]
    v = np.moveaxis(np.asarray(x, np.float32).astype(ml_dtypes.bfloat16).astype(np.float64), axis, -1)
    blocks = v.reshape(v.shape[:-1] + (-1, 32))
    amax = np.abs(blocks).max(-1, keepdims=True)
    byte = np.maximum(np.where(amax > 0, np.frexp(amax)[1] - 1 + 127, 0) - down, 1)
    scale = np.exp2(byte - 127.0)
    codes = (blocks / scale).astype(np.float32).astype(dtype).astype(np.float64)
    return np.moveaxis((codes * scale).reshape(v.shape), -1, axis)


WIDE = False


def mx_kscale(k):
    if not WIDE:
        return np.ones(k)
    levels = np.array([10, -10, 5, -5, 0])
    if k % 512:
        return np.exp2(np.random.permutation(np.resize(levels, k // 32))).repeat(32)
    a = np.empty((k // 512, 16))
    for p in range(k // 512):
        a[p, :8] = np.random.permutation(np.resize(levels, 8))
        for g in range(8):
            far = levels[np.abs(levels - a[p, g]) >= 10]
            a[p, g + 8] = far[np.random.randint(len(far))]
    return np.exp2(a.ravel()).repeat(32)


def f64(x):
    return np.asarray(x).astype(np.float64)


def striped(idx):
    return np.tile(idx.reshape(-1, 16).T, (8, 1)).astype(np.uint16)


def unstriped(offs):
    return offs[:16].T.reshape(-1).astype(np.int64)


def relu2(v):
    return np.maximum(v, 0.0) ** 2


K, T, E, C, N = 512, 768, 6, 256, 512


def by_expert(wq, xq):
    return np.concatenate([wq[e].T @ xq[:, e * C:(e + 1) * C] for e in range(E)], axis=1)


def setup_inputs():
    n = np.random.standard_normal
    s = mx_kscale(K)[:, None]
    first = np.random.permutation(np.repeat(np.arange(E), T // E))
    second = (first + 1 + np.random.permutation(np.repeat(np.arange(E - 1), -(-T // (E - 1)))[:T])) % E
    while np.bincount(second, minlength=E).max() != T // E:
        load = np.bincount(second, minlength=E); hi, lo = int(load.argmax()), int(load.argmin())
        t = np.flatnonzero((second == hi) & (first != lo))[0]; second[t] = lo
    slot_token = np.empty(E * C, np.int64); pos = np.empty((2, T), np.int64); fill = np.zeros(E, np.int64)
    place = np.stack([np.random.permutation(C) for _ in range(E)])
    for r, deal in enumerate((first, second)):
        for t in np.random.permutation(T):
            e = deal[t]; j = e * C + place[e, fill[e]]; fill[e] += 1; slot_token[j] = t; pos[r, t] = j
    g = np.random.uniform(0.2, 0.8, T)
    return {
        "xT": (n((K, T)) * s).astype(np.float32),
        "w": (n((E, K, N)) / np.sqrt(K) / s[None]).astype(np.float32),
        "b": (0.3 * n((N, E))).astype(np.float32),
        "gate": np.stack([np.tile(g, (N, 1)), np.tile(1.0 - g, (N, 1))]).astype(np.float32),
        "offs": striped(slot_token),
        "pos1": striped(pos[0]),
        "pos2": striped(pos[1]),
    }


def reference(xT, w, b, gate, offs, pos1, pos2):
    idx = unstriped(offs)
    xq = mxq(f64(xT)[:, idx], 0, "e4m3")
    y = by_expert(mxq(f64(w), 1, "e4m3"), xq)
    y = relu2(y + np.repeat(f64(b), C, axis=1))
    return f64(gate[0]) * y[:, unstriped(pos1)] + f64(gate[1]) * y[:, unstriped(pos2)]

@@ -1,0 +1,191 @@
+from contextlib import ExitStack
+
+import concourse.mybir as mybir
+
+K, T, E, C, N = 512, 768, 6, 256, 512
+FLOPS = 2 * K * N * E * C
+
+F32 = mybir.dt.float32
+BF16 = mybir.dt.bfloat16
+U32 = mybir.dt.uint32
+U16 = mybir.dt.uint16
+U8 = mybir.dt.uint8
+FP8X4 = mybir.dt.float8_e4m3fn_x4
+RELU = mybir.ActivationFunctionType.Relu
+SQUARE = mybir.ActivationFunctionType.Square
+MULT = mybir.AluOpType.mult
+ADD = mybir.AluOpType.add
+
+P = 128
+PACK = 4
+HALF = 256
+PIECE = 512
+
+
+def tile_routed_moe_kernel(tc, xT, w, b, gate, offs, pos1, pos2, out):
+    nc = tc.nc
+
+    def wide(raw, lo, hi):
+        return raw[:, :, lo:hi].rearrange("p t (c i) -> p c t i", i=4)
+
+    def packed(bf, lo, hi):
+        return bf[:, lo:hi, :].rearrange("p (c i) t -> p c t i", i=4)
+
+    with ExitStack() as ctx:
+        keep = ctx.enter_context(tc.tile_pool(name="keep", bufs=1))
+        work = ctx.enter_context(tc.tile_pool(name="work", bufs=2))
+        psum = ctx.enter_context(tc.psum_pool(name="psum", bufs=8))
+
+        offs_t = keep.tile([P, E * C // 16], U16, name="offs_t")
+        pos1_t = keep.tile([P, T // 16], U16, name="pos1_t")
+        pos2_t = keep.tile([P, T // 16], U16, name="pos2_t")
+        bias = keep.tile([P, N // P, E], F32, name="bias")
+
+        x_codes = keep.tile([P, T], U32, name="x_codes", align_bytes=64)
+        x_scales = keep.tile([P, T], U8, name="x_scales", align_bytes=64)
+        nc.gpsimd.memset(x_scales[:], 0)
+
+        x_cuts = [(0, 512, 352), (512, 768, 160)]
+        x_raw, x_bf = [], []
+        for lo, hi, split in x_cuts:
+            raw = keep.tile([P, PACK, hi - lo], F32, name=f"x_raw{lo}")
+            nc.sync.dma_start(raw[:], xT[:, lo:hi].rearrange("(p t) n -> p t n", t=PACK))
+            x_raw.append(raw)
+            x_bf.append(keep.tile([P, hi - lo, PACK], BF16, name=f"x_bf{lo}", align_bytes=64))
+        nc.sync.dma_start(offs_t[:], offs)
+        nc.scalar.dma_start(bias[:], b.rearrange("(f p) e -> p f e", p=P))
+
+        w_raw, gates = {}, {}
+
+        def load_w(e, h):
+            t = keep.tile([P, PACK, HALF], F32, name=f"w_raw{e}_{h}")
+            nc.sync.dma_start(t[:], w[e, :, h * HALF : (h + 1) * HALF].rearrange("(p t) n -> p t n", t=PACK))
+            w_raw[e, h] = t
+
+        def load_gate(f):
+            for r in range(2):
+                t = keep.tile([P, T], F32, name=f"gate{f}_{r}")
+                nc.sync.dma_start(t[:], gate[r, f * P : (f + 1) * P, :])
+                gates[f, r] = t
+
+        for e in range(E):
+            load_w(e, 0)
+        nc.sync.dma_start(pos1_t[:], pos1)
+        nc.sync.dma_start(pos2_t[:], pos2)
+        load_gate(0)
+        load_w(0, 1)
+        load_w(1, 1)
+        load_gate(1)
+        for e in range(2, E):
+            load_w(e, 1)
+        load_gate(2)
+        load_gate(3)
+
+        for (lo, hi, split), raw, bf in zip(x_cuts, x_raw, x_bf):
+            n = hi - lo
+            nc.vector.tensor_copy(packed(bf, 0, split), wide(raw, 0, split))
+            nc.scalar.copy(packed(bf, split, n), wide(raw, split, n))
+            nc.vector.quantize_mx(
+                out=x_codes[:, lo:hi].bitcast(FP8X4),
+                scales=x_scales[:, lo:hi],
+                in_=bf[:].rearrange("p n t -> p (n t)"),
+            )
+
+        g_codes, g_scales = [], []
+
+        def gather(i):
+            cols = slice(i * PIECE // 16, (i + 1) * PIECE // 16)
+            gc = keep.tile([P, PIECE], U32, name=f"g_codes{i}", align_bytes=64)
+            nc.vector.tensor_copy(gc[:], x_codes[:].indirect(offs_t[:, cols]))
+            gs = keep.tile([P, PIECE], U8, name=f"g_scales{i}", align_bytes=64)
+            nc.vector.tensor_copy(gs[:], x_scales[:].indirect(offs_t[:, cols]))
+            g_codes.append(gc)
+            g_scales.append(gs)
+
+        w_bf, w_codes, w_scales = {}, {}, {}
+
+        def interleave_w(e, h, on_gpsimd):
+            bf = keep.tile([P, HALF, PACK], BF16, name=f"w_bf{e}_{h}", align_bytes=64)
+            raw = w_raw[e, h]
+            if on_gpsimd:
+                nc.gpsimd.tensor_scalar(packed(bf, 0, HALF), wide(raw, 0, HALF), 1.0, 0.0, MULT, ADD)
+            else:
+                nc.scalar.copy(packed(bf, 0, HALF), wide(raw, 0, HALF))
+            w_bf[e, h] = bf
+
+        def quantise_w(e, h):
+            codes = keep.tile([P, HALF], U32, name=f"w_codes{e}_{h}", align_bytes=64)
+            scales = keep.tile([P, HALF], U8, name=f"w_scales{e}_{h}", align_bytes=64)
+            nc.vector.quantize_mx(
+                out=codes[:].bitcast(FP8X4), scales=scales[:], in_=w_bf[e, h][:].rearrange("p n t -> p (n t)")
+            )
+            w_codes[e, h] = codes
+            w_scales[e, h] = scales
+
+        y = [keep.tile([P, E * C], F32, name=f"y{f}") for f in range(N // P)]
+
+        def multiply(i, f):
+            acc = psum.tile([P, PIECE], F32, name="acc")
+            r = work.tile([P, PIECE], F32, name="r", bufs=4)
+            h, m = f // 2, slice((f % 2) * P, (f % 2 + 1) * P)
+            for s in range(2):
+                e, cols = 2 * i + s, slice(s * C, (s + 1) * C)
+                nc.tensor.matmul_mx(
+                    out=acc[:, cols],
+                    lhsT=w_codes[e, h][:, m].bitcast(FP8X4),
+                    lhsT_scale=w_scales[e, h][:, m],
+                    rhs=g_codes[i][:, cols].bitcast(FP8X4),
+                    rhs_scale=g_scales[i][:, cols],
+                    start=True,
+                    stop=True,
+                )
+            for s in range(2):
+                e, cols = 2 * i + s, slice(s * C, (s + 1) * C)
+                nc.scalar.activation(r[:, cols], acc[:, cols], RELU, bias=bias[:, f, e : e + 1])
+            nc.scalar.activation(y[f][:, i * PIECE : (i + 1) * PIECE], r[:], SQUARE)
+
+        def fetch(f):
+            parts = []
+            for r, pos in enumerate((pos1_t, pos2_t)):
+                t = work.tile([P, T], F32, name=f"part{r}")
+                nc.vector.tensor_tensor(t[:], y[f][:].indirect(pos[:]), gates[f, r][:], MULT)
+                parts.append(t)
+            return parts
+
+        def combine(f, parts):
+            o = work.tile([P, T], F32, name="o")
+            nc.vector.tensor_tensor(o[:], parts[0][:], parts[1][:], ADD)
+            nc.sync.dma_start(out[f * P : (f + 1) * P, :], o[:])
+
+        for e in range(E):
+            interleave_w(e, 0, e % 3 == 2)
+        gather(0)
+        quantise_w(0, 0)
+        quantise_w(1, 0)
+        gather(1)
+        quantise_w(2, 0)
+        quantise_w(3, 0)
+        gather(2)
+        quantise_w(4, 0)
+        quantise_w(5, 0)
+        for i in range(3):
+            multiply(i, 0)
+        for i in range(3):
+            multiply(i, 1)
+        for e in range(E):
+            interleave_w(e, 1, False)
+        p0 = fetch(0)
+        for e in range(3):
+            quantise_w(e, 1)
+        combine(0, p0)
+        p1 = fetch(1)
+        for e in range(3, E):
+            quantise_w(e, 1)
+        combine(1, p1)
+        for f in (2, 3):
+            for i in range(3):
+                multiply(i, f)
+        p2 = fetch(2)
+        combine(2, p2)
+        p3 = fetch(3)
+        combine(3, p3)

@@ -18,8 +18,8 @@ ADD = mybir.AluOpType.add
 
 P = 128
 PACK = 4
-HALF = 256
 PIECE = 512
+GPS = 128
 
 
 def tile_routed_moe_kernel(tc, xT, w, b, gate, offs, pos1, pos2, out):
@@ -57,10 +57,10 @@ def tile_routed_moe_kernel(tc, xT, w, b, gate, offs, pos1, pos2, out):
 
         w_raw, gates = {}, {}
 
-        def load_w(e, h):
-            t = keep.tile([P, PACK, HALF], F32, name=f"w_raw{e}_{h}")
-            nc.sync.dma_start(t[:], w[e, :, h * HALF : (h + 1) * HALF].rearrange("(p t) n -> p t n", t=PACK))
-            w_raw[e, h] = t
+        def load_w(e, lo, hi):
+            t = keep.tile([P, PACK, hi - lo], F32, name=f"w_raw{e}_{lo}")
+            nc.sync.dma_start(t[:], w[e, :, lo:hi].rearrange("(p t) n -> p t n", t=PACK))
+            w_raw[e, lo] = t
 
         def load_gate(f):
             for r in range(2):
@@ -68,18 +68,17 @@ def tile_routed_moe_kernel(tc, xT, w, b, gate, offs, pos1, pos2, out):
                 nc.sync.dma_start(t[:], gate[r, f * P : (f + 1) * P, :])
                 gates[f, r] = t
 
-        for e in range(E):
-            load_w(e, 0)
+        for e in range(4):
+            load_w(e, 0, N)
+        load_w(4, 0, 256)
+        load_w(5, 0, 256)
         nc.sync.dma_start(pos1_t[:], pos1)
         nc.sync.dma_start(pos2_t[:], pos2)
         load_gate(0)
-        load_w(0, 1)
-        load_w(1, 1)
-        load_gate(1)
-        for e in range(2, E):
-            load_w(e, 1)
-        load_gate(2)
-        load_gate(3)
+        load_w(4, 256, N)
+        load_w(5, 256, N)
+        for f in range(1, N // P):
+            load_gate(f)
 
         for (lo, hi, split), raw, bf in zip(x_cuts, x_raw, x_bf):
             n = hi - lo
@@ -102,38 +101,40 @@ def tile_routed_moe_kernel(tc, xT, w, b, gate, offs, pos1, pos2, out):
             g_codes.append(gc)
             g_scales.append(gs)
 
-        w_bf, w_codes, w_scales = {}, {}, {}
+        w_bf, w_of = {}, {}
 
-        def interleave_w(e, h, on_gpsimd):
-            bf = keep.tile([P, HALF, PACK], BF16, name=f"w_bf{e}_{h}", align_bytes=64)
-            raw = w_raw[e, h]
-            if on_gpsimd:
-                nc.gpsimd.tensor_scalar(packed(bf, 0, HALF), wide(raw, 0, HALF), 1.0, 0.0, MULT, ADD)
-            else:
-                nc.scalar.copy(packed(bf, 0, HALF), wide(raw, 0, HALF))
-            w_bf[e, h] = bf
+        def interleave_w(e, lo, hi):
+            n = hi - lo
+            bf = keep.tile([P, n, PACK], BF16, name=f"w_bf{e}_{lo}", align_bytes=64)
+            raw = w_raw[e, lo]
+            mine = n - GPS * n // N
+            if mine < n:
+                nc.gpsimd.tensor_scalar(packed(bf, mine, n), wide(raw, mine, n), 1.0, 0.0, MULT, ADD)
+            nc.scalar.copy(packed(bf, 0, mine), wide(raw, 0, mine))
+            w_bf[e, lo] = bf
 
-        def quantise_w(e, h):
-            codes = keep.tile([P, HALF], U32, name=f"w_codes{e}_{h}", align_bytes=64)
-            scales = keep.tile([P, HALF], U8, name=f"w_scales{e}_{h}", align_bytes=64)
+        def quantise_w(e, lo, hi):
+            n = hi - lo
+            codes = keep.tile([P, n], U32, name=f"w_codes{e}_{lo}", align_bytes=64)
+            scales = keep.tile([P, n], U8, name=f"w_scales{e}_{lo}", align_bytes=64)
             nc.vector.quantize_mx(
-                out=codes[:].bitcast(FP8X4), scales=scales[:], in_=w_bf[e, h][:].rearrange("p n t -> p (n t)")
+                out=codes[:].bitcast(FP8X4), scales=scales[:], in_=w_bf[e, lo][:].rearrange("p n t -> p (n t)")
             )
-            w_codes[e, h] = codes
-            w_scales[e, h] = scales
+            for f in range(lo // P, hi // P):
+                w_of[e, f] = (codes, scales, slice(f * P - lo, f * P - lo + P))
 
         y = [keep.tile([P, E * C], F32, name=f"y{f}") for f in range(N // P)]
 
         def multiply(i, f):
             acc = psum.tile([P, PIECE], F32, name="acc")
             r = work.tile([P, PIECE], F32, name="r", bufs=4)
-            h, m = f // 2, slice((f % 2) * P, (f % 2 + 1) * P)
             for s in range(2):
                 e, cols = 2 * i + s, slice(s * C, (s + 1) * C)
+                codes, scales, m = w_of[e, f]
                 nc.tensor.matmul_mx(
                     out=acc[:, cols],
-                    lhsT=w_codes[e, h][:, m].bitcast(FP8X4),
-                    lhsT_scale=w_scales[e, h][:, m],
+                    lhsT=codes[:, m].bitcast(FP8X4),
+                    lhsT_scale=scales[:, m],
                     rhs=g_codes[i][:, cols].bitcast(FP8X4),
                     rhs_scale=g_scales[i][:, cols],
                     start=True,
@@ -157,35 +158,35 @@ def tile_routed_moe_kernel(tc, xT, w, b, gate, offs, pos1, pos2, out):
             nc.vector.tensor_tensor(o[:], parts[0][:], parts[1][:], ADD)
             nc.sync.dma_start(out[f * P : (f + 1) * P, :], o[:])
 
-        for e in range(E):
-            interleave_w(e, 0, e % 3 == 2)
         gather(0)
-        quantise_w(0, 0)
-        quantise_w(1, 0)
+        for e in range(2):
+            interleave_w(e, 0, N)
+            quantise_w(e, 0, N)
+        multiply(0, 0)
         gather(1)
-        quantise_w(2, 0)
-        quantise_w(3, 0)
+        for e in range(2, 4):
+            interleave_w(e, 0, N)
+            quantise_w(e, 0, N)
+        multiply(1, 0)
         gather(2)
-        quantise_w(4, 0)
-        quantise_w(5, 0)
-        for i in range(3):
-            multiply(i, 0)
+        for e in range(4, 6):
+            interleave_w(e, 0, 256)
+            quantise_w(e, 0, 256)
+        multiply(2, 0)
+        p0 = fetch(0)
         for i in range(3):
             multiply(i, 1)
-        for e in range(E):
-            interleave_w(e, 1, False)
-        p0 = fetch(0)
-        for e in range(3):
-            quantise_w(e, 1)
+        for e in range(4, 6):
+            interleave_w(e, 256, N)
+            quantise_w(e, 256, N)
         combine(0, p0)
         p1 = fetch(1)
-        for e in range(3, E):
-            quantise_w(e, 1)
+        for i in range(3):
+            multiply(i, 2)
         combine(1, p1)
-        for f in (2, 3):
-            for i in range(3):
-                multiply(i, f)
         p2 = fetch(2)
+        for i in range(3):
+            multiply(i, 3)
         combine(2, p2)
         p3 = fetch(3)
         combine(3, p3)

@@ -1,6 +1,7 @@
 from contextlib import ExitStack
 
 import concourse.mybir as mybir
+from concourse.masks import make_identity
 
 K, T, E, C, N = 512, 768, 6, 256, 512
 FLOPS = 2 * K * N * E * C
@@ -19,7 +20,10 @@ ADD = mybir.AluOpType.add
 P = 128
 PACK = 4
 PIECE = 512
-GPS = 128
+TAG_CODES = ["g_codes0","g_codes1","w_bf1"]
+TAG_SCALES = ["g_scales0","w_bf0","w_bf2"]
+V_COLS = [0,64,128,160,192,144,0]
+G_COLS = [0,0,0,0,0,0,0]
 
 
 def tile_routed_moe_kernel(tc, xT, w, b, gate, offs, pos1, pos2, out):
@@ -34,7 +38,7 @@ def tile_routed_moe_kernel(tc, xT, w, b, gate, offs, pos1, pos2, out):
     with ExitStack() as ctx:
         keep = ctx.enter_context(tc.tile_pool(name="keep", bufs=1))
         work = ctx.enter_context(tc.tile_pool(name="work", bufs=2))
-        psum = ctx.enter_context(tc.psum_pool(name="psum", bufs=8))
+        psum = ctx.enter_context(tc.psum_pool(name="psum", bufs=6))
 
         offs_t = keep.tile([P, E * C // 16], U16, name="offs_t")
         pos1_t = keep.tile([P, T // 16], U16, name="pos1_t")
@@ -44,6 +48,9 @@ def tile_routed_moe_kernel(tc, xT, w, b, gate, offs, pos1, pos2, out):
         x_codes = keep.tile([P, T], U32, name="x_codes", align_bytes=64)
         x_scales = keep.tile([P, T], U8, name="x_scales", align_bytes=64)
         nc.gpsimd.memset(x_scales[:], 0)
+
+        ident = keep.tile([P, P], F32, name="ident")
+        make_identity(nc, ident[:])
 
         x_cuts = [(0, 512, 352), (512, 768, 160)]
         x_raw, x_bf = [], []
@@ -68,16 +75,13 @@ def tile_routed_moe_kernel(tc, xT, w, b, gate, offs, pos1, pos2, out):
                 nc.sync.dma_start(t[:], gate[r, f * P : (f + 1) * P, :])
                 gates[f, r] = t
 
-        for e in range(4):
+        for e in range(E - 1):
             load_w(e, 0, N)
-        load_w(4, 0, 256)
         load_w(5, 0, 256)
+        load_w(5, 256, N)
         nc.sync.dma_start(pos1_t[:], pos1)
         nc.sync.dma_start(pos2_t[:], pos2)
-        load_gate(0)
-        load_w(4, 256, N)
-        load_w(5, 256, N)
-        for f in range(1, N // P):
+        for f in range(N // P):
             load_gate(f)
 
         for (lo, hi, split), raw, bf in zip(x_cuts, x_raw, x_bf):
@@ -94,9 +98,9 @@ def tile_routed_moe_kernel(tc, xT, w, b, gate, offs, pos1, pos2, out):
 
         def gather(i):
             cols = slice(i * PIECE // 16, (i + 1) * PIECE // 16)
-            gc = keep.tile([P, PIECE], U32, name=f"g_codes{i}", align_bytes=64)
+            gc = keep.tile([P, PIECE], U32, name=f"g_codes{i}", tag=TAG_CODES[i], align_bytes=64)
             nc.vector.tensor_copy(gc[:], x_codes[:].indirect(offs_t[:, cols]))
-            gs = keep.tile([P, PIECE], U8, name=f"g_scales{i}", align_bytes=64)
+            gs = keep.tile([P, PIECE], U8, name=f"g_scales{i}", tag=TAG_SCALES[i], align_bytes=64)
             nc.vector.tensor_copy(gs[:], x_scales[:].indirect(offs_t[:, cols]))
             g_codes.append(gc)
             g_scales.append(gs)
@@ -105,12 +109,15 @@ def tile_routed_moe_kernel(tc, xT, w, b, gate, offs, pos1, pos2, out):
 
         def interleave_w(e, lo, hi):
             n = hi - lo
-            bf = keep.tile([P, n, PACK], BF16, name=f"w_bf{e}_{lo}", align_bytes=64)
+            bf = keep.tile([P, n, PACK], BF16, name=f"w_bf{e}" if lo == 0 else "w_bf_last", align_bytes=64)
             raw = w_raw[e, lo]
-            mine = n - GPS * n // N
-            if mine < n:
-                nc.gpsimd.tensor_scalar(packed(bf, mine, n), wide(raw, mine, n), 1.0, 0.0, MULT, ADD)
+            j = e if lo == 0 else E
+            mine = n - V_COLS[j] - G_COLS[j]
             nc.scalar.copy(packed(bf, 0, mine), wide(raw, 0, mine))
+            if V_COLS[j]:
+                nc.vector.tensor_copy(packed(bf, mine, mine + V_COLS[j]), wide(raw, mine, mine + V_COLS[j]))
+            if G_COLS[j]:
+                nc.gpsimd.tensor_scalar(packed(bf, n - G_COLS[j], n), wide(raw, n - G_COLS[j], n), 1.0, 0.0, MULT, ADD)
             w_bf[e, lo] = bf
 
         def quantise_w(e, lo, hi):
@@ -145,48 +152,63 @@ def tile_routed_moe_kernel(tc, xT, w, b, gate, offs, pos1, pos2, out):
                 nc.scalar.activation(r[:, cols], acc[:, cols], RELU, bias=bias[:, f, e : e + 1])
             nc.scalar.activation(y[f][:, i * PIECE : (i + 1) * PIECE], r[:], SQUARE)
 
-        def fetch(f):
-            parts = []
-            for r, pos in enumerate((pos1_t, pos2_t)):
-                t = work.tile([P, T], F32, name=f"part{r}")
-                nc.vector.tensor_tensor(t[:], y[f][:].indirect(pos[:]), gates[f, r][:], MULT)
-                parts.append(t)
-            return parts
+        def fetch(f, r, lo, hi):
+            pos = (pos1_t, pos2_t)[r]
+            t = work.tile([P, hi - lo], F32, name=f"part{r}_{lo}_{hi}", bufs=2)
+            offsets = pos[:, lo // 16 : hi // 16]
+            nc.vector.tensor_tensor(t[:], y[f][:].indirect(offsets), gates[f, r][:, lo:hi], MULT)
+            return t
 
-        def combine(f, parts):
-            o = work.tile([P, T], F32, name="o")
-            nc.vector.tensor_tensor(o[:], parts[0][:], parts[1][:], ADD)
-            nc.sync.dma_start(out[f * P : (f + 1) * P, :], o[:])
+        def add_on_vector(f, parts, base, lo, hi):
+            o = work.tile([P, hi - lo], F32, name=f"o_{lo}_{hi}")
+            cut = slice(lo - base, hi - base)
+            nc.vector.tensor_tensor(o[:], parts[0][:, cut], parts[1][:, cut], ADD)
+            nc.sync.dma_start(out[f * P : (f + 1) * P, lo:hi], o[:])
+
+        def add_on_tensor(f, parts, lo, hi):
+            total = psum.tile([P, PIECE], F32, name="total", bufs=2)
+            o = work.tile([P, hi - lo], F32, name=f"o_{lo}_{hi}")
+            for r in range(2):
+                nc.tensor.matmul(total[:, : hi - lo], ident[:], parts[r][:, lo:hi], start=(r == 0), stop=(r == 1))
+            nc.scalar.copy(o[:], total[:, : hi - lo])
+            nc.sync.dma_start(out[f * P : (f + 1) * P, lo:hi], o[:])
 
         gather(0)
-        for e in range(2):
-            interleave_w(e, 0, N)
-            quantise_w(e, 0, N)
-        multiply(0, 0)
+        interleave_w(0, 0, N)
+        quantise_w(0, 0, N)
+        interleave_w(1, 0, N)
+        quantise_w(1, 0, N)
+        interleave_w(2, 0, N)
         gather(1)
-        for e in range(2, 4):
-            interleave_w(e, 0, N)
-            quantise_w(e, 0, N)
-        multiply(1, 0)
+        multiply(0, 0)
+        quantise_w(2, 0, N)
         gather(2)
-        for e in range(4, 6):
-            interleave_w(e, 0, 256)
-            quantise_w(e, 0, 256)
+        interleave_w(3, 0, N)
+        quantise_w(3, 0, N)
+        multiply(1, 0)
+        interleave_w(4, 0, N)
+        quantise_w(4, 0, N)
+        interleave_w(5, 0, 256)
+        quantise_w(5, 0, 256)
         multiply(2, 0)
-        p0 = fetch(0)
+        p0 = [fetch(0, r, 0, T) for r in range(2)]
         for i in range(3):
             multiply(i, 1)
-        for e in range(4, 6):
-            interleave_w(e, 256, N)
-            quantise_w(e, 256, N)
-        combine(0, p0)
-        p1 = fetch(1)
+        interleave_w(5, 256, N)
+        quantise_w(5, 256, N)
         for i in range(3):
             multiply(i, 2)
-        combine(1, p1)
-        p2 = fetch(2)
+        p1 = [fetch(1, r, 0, T) for r in range(2)]
         for i in range(3):
             multiply(i, 3)
-        combine(2, p2)
-        p3 = fetch(3)
-        combine(3, p3)
+        add_on_tensor(0, p0, 0, 512)
+        add_on_tensor(0, p0, 512, T)
+        p2 = [fetch(2, r, 0, T) for r in range(2)]
+        add_on_vector(1, p1, 0, 448, T)
+        add_on_tensor(1, p1, 0, 448)
+        p3 = [fetch(3, r, 0, 512) for r in range(2)]
+        add_on_vector(2, p2, 0, 0, T)
+        q3 = [fetch(3, 0, 512, T)]
+        add_on_vector(3, p3, 0, 0, 512)
+        q3.append(fetch(3, 1, 512, T))
+        add_on_vector(3, q3, 512, 512, T)

@@ -19,196 +19,212 @@ ADD = mybir.AluOpType.add
 
 P = 128
 PACK = 4
-PIECE = 512
-TAG_CODES = ["g_codes0","g_codes1","w_bf1"]
-TAG_SCALES = ["g_scales0","w_bf0","w_bf2"]
-V_COLS = [0,64,128,160,192,144,0]
-G_COLS = [0,0,0,0,0,0,0]
+BLOCKS = N // P
+PAIRS = E // 2
+PAIR = 2 * C
+OFFSETS_A_COLUMN = 16
+
+CHUNKS = [(0, 512, 352), (512, T, 160)]
+
+HALF = N // 2
+STRIPS = [(0, 0, N), (1, 0, N), (2, 0, N), (3, 0, N), (4, 0, HALF), (5, 0, HALF), (4, HALF, N), (5, HALF, N)]
+ON_VECTOR = {(2, 0): 128, (3, 0): 192, (4, 0): 192, (5, 0): 176, (4, HALF): 192, (5, HALF): 192}
+
+GATHER_AFTER = {("scales", 1): 0, ("codes", 2): 1, ("scales", 2): 2}
+
+SUMS_ON_TENSOR = [(0, 0, 512), (0, 512, T), (1, 0, 448)]
+LAST_CUT = 512
 
 
 def tile_routed_moe_kernel(tc, xT, w, b, gate, offs, pos1, pos2, out):
     nc = tc.nc
 
-    def wide(raw, lo, hi):
+    def planes(raw, lo, hi):
         return raw[:, :, lo:hi].rearrange("p t (c i) -> p c t i", i=4)
 
-    def packed(bf, lo, hi):
-        return bf[:, lo:hi, :].rearrange("p (c i) t -> p c t i", i=4)
+    def words(packed, lo, hi):
+        return packed[:, lo:hi, :].rearrange("p (c i) t -> p c t i", i=4)
 
     with ExitStack() as ctx:
         keep = ctx.enter_context(tc.tile_pool(name="keep", bufs=1))
         work = ctx.enter_context(tc.tile_pool(name="work", bufs=2))
         psum = ctx.enter_context(tc.psum_pool(name="psum", bufs=6))
 
-        offs_t = keep.tile([P, E * C // 16], U16, name="offs_t")
-        pos1_t = keep.tile([P, T // 16], U16, name="pos1_t")
-        pos2_t = keep.tile([P, T // 16], U16, name="pos2_t")
-        bias = keep.tile([P, N // P, E], F32, name="bias")
+        offs_list = keep.tile([P, E * C // OFFSETS_A_COLUMN], U16, name="offs_list")
+        pos_lists = [keep.tile([P, T // OFFSETS_A_COLUMN], U16, name=f"pos_list{r}") for r in range(2)]
+        bias = keep.tile([P, BLOCKS, E], F32, name="bias")
 
         x_codes = keep.tile([P, T], U32, name="x_codes", align_bytes=64)
         x_scales = keep.tile([P, T], U8, name="x_scales", align_bytes=64)
         nc.gpsimd.memset(x_scales[:], 0)
+        identity = keep.tile([P, P], F32, name="identity")
+        make_identity(nc, identity[:])
 
-        ident = keep.tile([P, P], F32, name="ident")
-        make_identity(nc, ident[:])
-
-        x_cuts = [(0, 512, 352), (512, 768, 160)]
-        x_raw, x_bf = [], []
-        for lo, hi, split in x_cuts:
+        x_raw = []
+        for lo, hi, split in CHUNKS:
             raw = keep.tile([P, PACK, hi - lo], F32, name=f"x_raw{lo}")
             nc.sync.dma_start(raw[:], xT[:, lo:hi].rearrange("(p t) n -> p t n", t=PACK))
             x_raw.append(raw)
-            x_bf.append(keep.tile([P, hi - lo, PACK], BF16, name=f"x_bf{lo}", align_bytes=64))
-        nc.sync.dma_start(offs_t[:], offs)
+        nc.sync.dma_start(offs_list[:], offs)
         nc.scalar.dma_start(bias[:], b.rearrange("(f p) e -> p f e", p=P))
 
-        w_raw, gates = {}, {}
+        w_raw = {}
 
-        def load_w(e, lo, hi):
-            t = keep.tile([P, PACK, hi - lo], F32, name=f"w_raw{e}_{lo}")
-            nc.sync.dma_start(t[:], w[e, :, lo:hi].rearrange("(p t) n -> p t n", t=PACK))
-            w_raw[e, lo] = t
+        def load_weights(e, lo, hi):
+            raw = keep.tile([P, PACK, hi - lo], F32, name=f"w_raw{e}_{lo}")
+            nc.sync.dma_start(raw[:], w[e, :, lo:hi].rearrange("(p t) n -> p t n", t=PACK))
+            w_raw[e, lo] = raw
 
-        def load_gate(f):
+        load_weights(0, 0, HALF)
+        load_weights(0, HALF, N)
+        for e, lo, hi in STRIPS[1:]:
+            load_weights(e, lo, hi)
+
+        gates = {}
+
+        def load_gate(f, r):
+            gates[f, r] = keep.tile([P, T], F32, name=f"gate{f}_{r}")
+            nc.sync.dma_start(gates[f, r][:], gate[r, f * P : (f + 1) * P, :])
+
+        nc.sync.dma_start(pos_lists[0][:], pos1)
+        load_gate(0, 0)
+        nc.sync.dma_start(pos_lists[1][:], pos2)
+        load_gate(0, 1)
+        for f in range(1, BLOCKS):
             for r in range(2):
-                t = keep.tile([P, T], F32, name=f"gate{f}_{r}")
-                nc.sync.dma_start(t[:], gate[r, f * P : (f + 1) * P, :])
-                gates[f, r] = t
+                load_gate(f, r)
 
-        for e in range(E - 1):
-            load_w(e, 0, N)
-        load_w(5, 0, 256)
-        load_w(5, 256, N)
-        nc.sync.dma_start(pos1_t[:], pos1)
-        nc.sync.dma_start(pos2_t[:], pos2)
-        for f in range(N // P):
-            load_gate(f)
-
-        for (lo, hi, split), raw, bf in zip(x_cuts, x_raw, x_bf):
-            n = hi - lo
-            nc.vector.tensor_copy(packed(bf, 0, split), wide(raw, 0, split))
-            nc.scalar.copy(packed(bf, split, n), wide(raw, split, n))
+        for raw, (lo, hi, split) in zip(x_raw, CHUNKS):
+            packed = keep.tile([P, hi - lo, PACK], BF16, name=f"x_packed{lo}", align_bytes=64)
+            nc.vector.tensor_copy(words(packed, 0, split), planes(raw, 0, split))
+            nc.scalar.copy(words(packed, split, hi - lo), planes(raw, split, hi - lo))
             nc.vector.quantize_mx(
                 out=x_codes[:, lo:hi].bitcast(FP8X4),
                 scales=x_scales[:, lo:hi],
-                in_=bf[:].rearrange("p n t -> p (n t)"),
+                in_=packed[:].rearrange("p n t -> p (n t)"),
             )
 
-        g_codes, g_scales = [], []
+        slot_codes, slot_scales = {}, {}
 
         def gather(i):
-            cols = slice(i * PIECE // 16, (i + 1) * PIECE // 16)
-            gc = keep.tile([P, PIECE], U32, name=f"g_codes{i}", tag=TAG_CODES[i], align_bytes=64)
-            nc.vector.tensor_copy(gc[:], x_codes[:].indirect(offs_t[:, cols]))
-            gs = keep.tile([P, PIECE], U8, name=f"g_scales{i}", tag=TAG_SCALES[i], align_bytes=64)
-            nc.vector.tensor_copy(gs[:], x_scales[:].indirect(offs_t[:, cols]))
-            g_codes.append(gc)
-            g_scales.append(gs)
+            columns = PAIR // OFFSETS_A_COLUMN
+            offsets = offs_list[:, i * columns : (i + 1) * columns]
+            for kind, dtype, window, slots in (
+                ("codes", U32, x_codes, slot_codes),
+                ("scales", U8, x_scales, slot_scales),
+            ):
+                after = GATHER_AFTER.get((kind, i))
+                tag = f"slot_{kind}{i}" if after is None else f"w_packed{after}_0"
+                slots[i] = keep.tile([P, PAIR], dtype, name=f"slot_{kind}{i}", tag=tag, align_bytes=64)
+                nc.vector.tensor_copy(slots[i][:], window[:].indirect(offsets))
 
-        w_bf, w_of = {}, {}
+        w_block = {}
 
-        def interleave_w(e, lo, hi):
-            n = hi - lo
-            bf = keep.tile([P, n, PACK], BF16, name=f"w_bf{e}" if lo == 0 else "w_bf_last", align_bytes=64)
-            raw = w_raw[e, lo]
-            j = e if lo == 0 else E
-            mine = n - V_COLS[j] - G_COLS[j]
-            nc.scalar.copy(packed(bf, 0, mine), wide(raw, 0, mine))
-            if V_COLS[j]:
-                nc.vector.tensor_copy(packed(bf, mine, mine + V_COLS[j]), wide(raw, mine, mine + V_COLS[j]))
-            if G_COLS[j]:
-                nc.gpsimd.tensor_scalar(packed(bf, n - G_COLS[j], n), wide(raw, n - G_COLS[j], n), 1.0, 0.0, MULT, ADD)
-            w_bf[e, lo] = bf
+        def prepare(strip):
+            e, lo, hi = strip
+            packed = keep.tile([P, hi - lo, PACK], BF16, name=f"w_packed{e}_{lo}", align_bytes=64)
+            if e == 0:
+                for half in (0, HALF):
+                    nc.scalar.copy(words(packed, half, half + HALF), planes(w_raw[e, half], 0, HALF))
+            else:
+                split = hi - lo - ON_VECTOR.get((e, lo), 0)
+                nc.scalar.copy(words(packed, 0, split), planes(w_raw[e, lo], 0, split))
+                if split < hi - lo:
+                    nc.vector.tensor_copy(words(packed, split, hi - lo), planes(w_raw[e, lo], split, hi - lo))
 
-        def quantise_w(e, lo, hi):
-            n = hi - lo
-            codes = keep.tile([P, n], U32, name=f"w_codes{e}_{lo}", align_bytes=64)
-            scales = keep.tile([P, n], U8, name=f"w_scales{e}_{lo}", align_bytes=64)
-            nc.vector.quantize_mx(
-                out=codes[:].bitcast(FP8X4), scales=scales[:], in_=w_bf[e, lo][:].rearrange("p n t -> p (n t)")
-            )
-            for f in range(lo // P, hi // P):
-                w_of[e, f] = (codes, scales, slice(f * P - lo, f * P - lo + P))
+            def quantise():
+                codes = keep.tile([P, hi - lo], U32, name=f"w_codes{e}_{lo}", align_bytes=64)
+                scales = keep.tile([P, hi - lo], U8, name=f"w_scales{e}_{lo}", align_bytes=64)
+                nc.vector.quantize_mx(
+                    out=codes[:].bitcast(FP8X4), scales=scales[:], in_=packed[:].rearrange("p n t -> p (n t)")
+                )
+                for f in range(lo // P, hi // P):
+                    w_block[e, f] = (codes, scales, slice(f * P - lo, (f + 1) * P - lo))
 
-        y = [keep.tile([P, E * C], F32, name=f"y{f}") for f in range(N // P)]
+            return quantise
+
+        y = [keep.tile([P, E * C], F32, name=f"y{f}") for f in range(BLOCKS)]
+        activated = {}
 
         def multiply(i, f):
-            acc = psum.tile([P, PIECE], F32, name="acc")
-            r = work.tile([P, PIECE], F32, name="r", bufs=4)
+            acc = psum.tile([P, PAIR], F32, name="acc")
             for s in range(2):
-                e, cols = 2 * i + s, slice(s * C, (s + 1) * C)
-                codes, scales, m = w_of[e, f]
+                slots = slice(s * C, (s + 1) * C)
+                codes, scales, features = w_block[2 * i + s, f]
                 nc.tensor.matmul_mx(
-                    out=acc[:, cols],
-                    lhsT=codes[:, m].bitcast(FP8X4),
-                    lhsT_scale=scales[:, m],
-                    rhs=g_codes[i][:, cols].bitcast(FP8X4),
-                    rhs_scale=g_scales[i][:, cols],
+                    out=acc[:, slots],
+                    lhsT=codes[:, features].bitcast(FP8X4),
+                    lhsT_scale=scales[:, features],
+                    rhs=slot_codes[i][:, slots].bitcast(FP8X4),
+                    rhs_scale=slot_scales[i][:, slots],
                     start=True,
                     stop=True,
                 )
+            first = i if f == 0 else 0
+            last = i if f == 0 else PAIRS - 1
+            width = (last - first + 1) * PAIR
+            if i == first:
+                activated[f] = work.tile([P, width], F32, name=f"activated{width}")
+            r = activated[f]
             for s in range(2):
-                e, cols = 2 * i + s, slice(s * C, (s + 1) * C)
-                nc.scalar.activation(r[:, cols], acc[:, cols], RELU, bias=bias[:, f, e : e + 1])
-            nc.scalar.activation(y[f][:, i * PIECE : (i + 1) * PIECE], r[:], SQUARE)
+                e = 2 * i + s
+                at = e * C - first * PAIR
+                nc.scalar.activation(r[:, at : at + C], acc[:, s * C : (s + 1) * C], RELU, bias=bias[:, f, e : e + 1])
+            if i == last:
+                nc.scalar.activation(y[f][:, first * PAIR : first * PAIR + width], r[:], SQUARE)
 
         def fetch(f, r, lo, hi):
-            pos = (pos1_t, pos2_t)[r]
-            t = work.tile([P, hi - lo], F32, name=f"part{r}_{lo}_{hi}", bufs=2)
-            offsets = pos[:, lo // 16 : hi // 16]
-            nc.vector.tensor_tensor(t[:], y[f][:].indirect(offsets), gates[f, r][:, lo:hi], MULT)
-            return t
+            part = work.tile([P, hi - lo], F32, name=f"part{r}_{lo}_{hi}")
+            offsets = pos_lists[r][:, lo // OFFSETS_A_COLUMN : hi // OFFSETS_A_COLUMN]
+            nc.vector.tensor_tensor(part[:], y[f][:].indirect(offsets), gates[f, r][:, lo:hi], MULT)
+            return part
 
-        def add_on_vector(f, parts, base, lo, hi):
-            o = work.tile([P, hi - lo], F32, name=f"o_{lo}_{hi}")
-            cut = slice(lo - base, hi - base)
-            nc.vector.tensor_tensor(o[:], parts[0][:, cut], parts[1][:, cut], ADD)
-            nc.sync.dma_start(out[f * P : (f + 1) * P, lo:hi], o[:])
-
-        def add_on_tensor(f, parts, lo, hi):
-            total = psum.tile([P, PIECE], F32, name="total", bufs=2)
-            o = work.tile([P, hi - lo], F32, name=f"o_{lo}_{hi}")
-            for r in range(2):
-                nc.tensor.matmul(total[:, : hi - lo], ident[:], parts[r][:, lo:hi], start=(r == 0), stop=(r == 1))
-            nc.scalar.copy(o[:], total[:, : hi - lo])
-            nc.sync.dma_start(out[f * P : (f + 1) * P, lo:hi], o[:])
+        def finish(f, parts, first, lo, hi):
+            total = work.tile([P, hi - lo], F32, name=f"total_{lo}_{hi}")
+            columns = slice(lo - first, hi - first)
+            if (f, lo, hi) in SUMS_ON_TENSOR:
+                bank = psum.tile([P, PAIR], F32, name="bank", bufs=2)
+                for r in range(2):
+                    nc.tensor.matmul(
+                        bank[:, : hi - lo], identity[:], parts[r][:, columns], start=(r == 0), stop=(r == 1)
+                    )
+                nc.scalar.copy(total[:], bank[:, : hi - lo])
+            else:
+                nc.vector.tensor_tensor(total[:], parts[0][:, columns], parts[1][:, columns], ADD)
+            nc.sync.dma_start(out[f * P : (f + 1) * P, lo:hi], total[:])
 
         gather(0)
-        interleave_w(0, 0, N)
-        quantise_w(0, 0, N)
-        interleave_w(1, 0, N)
-        quantise_w(1, 0, N)
-        interleave_w(2, 0, N)
+        prepare(STRIPS[0])()
+        prepare(STRIPS[1])()
+        quantise = prepare(STRIPS[2])
         gather(1)
         multiply(0, 0)
-        quantise_w(2, 0, N)
+        quantise()
         gather(2)
-        interleave_w(3, 0, N)
-        quantise_w(3, 0, N)
+        prepare(STRIPS[3])()
+        quantise = prepare(STRIPS[4])
         multiply(1, 0)
-        interleave_w(4, 0, N)
-        quantise_w(4, 0, N)
-        interleave_w(5, 0, 256)
-        quantise_w(5, 0, 256)
+        quantise()
+        prepare(STRIPS[5])()
         multiply(2, 0)
-        p0 = [fetch(0, r, 0, T) for r in range(2)]
-        for i in range(3):
-            multiply(i, 1)
-        interleave_w(5, 256, N)
-        quantise_w(5, 256, N)
-        for i in range(3):
-            multiply(i, 2)
-        p1 = [fetch(1, r, 0, T) for r in range(2)]
-        for i in range(3):
+        for strip in STRIPS[6:]:
+            prepare(strip)()
+
+        parts0 = [fetch(0, r, 0, T) for r in range(2)]
+        for f in (1, 2):
+            for i in range(PAIRS):
+                multiply(i, f)
+        parts1 = [fetch(1, r, 0, T) for r in range(2)]
+        for i in range(PAIRS):
             multiply(i, 3)
-        add_on_tensor(0, p0, 0, 512)
-        add_on_tensor(0, p0, 512, T)
-        p2 = [fetch(2, r, 0, T) for r in range(2)]
-        add_on_vector(1, p1, 0, 448, T)
-        add_on_tensor(1, p1, 0, 448)
-        p3 = [fetch(3, r, 0, 512) for r in range(2)]
-        add_on_vector(2, p2, 0, 0, T)
-        q3 = [fetch(3, 0, 512, T)]
-        add_on_vector(3, p3, 0, 0, 512)
-        q3.append(fetch(3, 1, 512, T))
-        add_on_vector(3, q3, 512, 512, T)
+        finish(0, parts0, 0, 0, 512)
+        finish(0, parts0, 0, 512, T)
+        parts2 = [fetch(2, r, 0, T) for r in range(2)]
+        finish(1, parts1, 0, 448, T)
+        finish(1, parts1, 0, 0, 448)
+        parts3 = [fetch(3, r, 0, LAST_CUT) for r in range(2)]
+        finish(2, parts2, 0, 0, T)
+        late = [fetch(3, 0, LAST_CUT, T)]
+        finish(3, parts3, 0, 0, LAST_CUT)
+        late.append(fetch(3, 1, LAST_CUT, T))
+        finish(3, late, LAST_CUT, LAST_CUT, T)

from contextlib import ExitStack

import concourse.mybir as mybir
from concourse.masks import make_identity

K, T, E, C, N = 512, 768, 6, 256, 512
FLOPS = 2 * K * N * E * C

F32 = mybir.dt.float32
BF16 = mybir.dt.bfloat16
U32 = mybir.dt.uint32
U16 = mybir.dt.uint16
U8 = mybir.dt.uint8
FP8X4 = mybir.dt.float8_e4m3fn_x4
RELU = mybir.ActivationFunctionType.Relu
SQUARE = mybir.ActivationFunctionType.Square
MULT = mybir.AluOpType.mult
ADD = mybir.AluOpType.add

P = 128
PACK = 4
BLOCKS = N // P
PAIRS = E // 2
PAIR = 2 * C
OFFSETS_A_COLUMN = 16

CHUNKS = [(0, 512, 352), (512, T, 160)]

HALF = N // 2
STRIPS = [(0, 0, N), (1, 0, N), (2, 0, N), (3, 0, N), (4, 0, HALF), (5, 0, HALF), (4, HALF, N), (5, HALF, N)]
ON_VECTOR = {(2, 0): 128, (3, 0): 192, (4, 0): 192, (5, 0): 176, (4, HALF): 192, (5, HALF): 192}

GATHER_AFTER = {("scales", 1): 0, ("codes", 2): 1, ("scales", 2): 2}

SUMS_ON_TENSOR = [(0, 0, 512), (0, 512, T), (1, 0, 448)]
LAST_CUT = 512


def tile_routed_moe_kernel(tc, xT, w, b, gate, offs, pos1, pos2, out):
    nc = tc.nc

    def planes(raw, lo, hi):
        return raw[:, :, lo:hi].rearrange("p t (c i) -> p c t i", i=4)

    def words(packed, lo, hi):
        return packed[:, lo:hi, :].rearrange("p (c i) t -> p c t i", i=4)

    with ExitStack() as ctx:
        keep = ctx.enter_context(tc.tile_pool(name="keep", bufs=1))
        work = ctx.enter_context(tc.tile_pool(name="work", bufs=2))
        psum = ctx.enter_context(tc.psum_pool(name="psum", bufs=6))

        offs_list = keep.tile([P, E * C // OFFSETS_A_COLUMN], U16, name="offs_list")
        pos_lists = [keep.tile([P, T // OFFSETS_A_COLUMN], U16, name=f"pos_list{r}") for r in range(2)]
        bias = keep.tile([P, BLOCKS, E], F32, name="bias")

        x_codes = keep.tile([P, T], U32, name="x_codes", align_bytes=64)
        x_scales = keep.tile([P, T], U8, name="x_scales", align_bytes=64)
        nc.gpsimd.memset(x_scales[:], 0)
        identity = keep.tile([P, P], F32, name="identity")
        make_identity(nc, identity[:])

        x_raw = []
        for lo, hi, split in CHUNKS:
            raw = keep.tile([P, PACK, hi - lo], F32, name=f"x_raw{lo}")
            nc.sync.dma_start(raw[:], xT[:, lo:hi].rearrange("(p t) n -> p t n", t=PACK))
            x_raw.append(raw)
        nc.sync.dma_start(offs_list[:], offs)
        nc.scalar.dma_start(bias[:], b.rearrange("(f p) e -> p f e", p=P))

        w_raw = {}

        def load_weights(e, lo, hi):
            raw = keep.tile([P, PACK, hi - lo], F32, name=f"w_raw{e}_{lo}")
            nc.sync.dma_start(raw[:], w[e, :, lo:hi].rearrange("(p t) n -> p t n", t=PACK))
            w_raw[e, lo] = raw

        load_weights(0, 0, HALF)
        load_weights(0, HALF, N)
        for e, lo, hi in STRIPS[1:]:
            load_weights(e, lo, hi)

        gates = {}

        def load_gate(f, r):
            gates[f, r] = keep.tile([P, T], F32, name=f"gate{f}_{r}")
            nc.sync.dma_start(gates[f, r][:], gate[r, f * P : (f + 1) * P, :])

        nc.sync.dma_start(pos_lists[0][:], pos1)
        load_gate(0, 0)
        nc.sync.dma_start(pos_lists[1][:], pos2)
        load_gate(0, 1)
        for f in range(1, BLOCKS):
            for r in range(2):
                load_gate(f, r)

        for raw, (lo, hi, split) in zip(x_raw, CHUNKS):
            packed = keep.tile([P, hi - lo, PACK], BF16, name=f"x_packed{lo}", align_bytes=64)
            nc.vector.tensor_copy(words(packed, 0, split), planes(raw, 0, split))
            nc.scalar.copy(words(packed, split, hi - lo), planes(raw, split, hi - lo))
            nc.vector.quantize_mx(
                out=x_codes[:, lo:hi].bitcast(FP8X4),
                scales=x_scales[:, lo:hi],
                in_=packed[:].rearrange("p n t -> p (n t)"),
            )

        slot_codes, slot_scales = {}, {}

        def gather(i):
            columns = PAIR // OFFSETS_A_COLUMN
            offsets = offs_list[:, i * columns : (i + 1) * columns]
            for kind, dtype, window, slots in (
                ("codes", U32, x_codes, slot_codes),
                ("scales", U8, x_scales, slot_scales),
            ):
                after = GATHER_AFTER.get((kind, i))
                tag = f"slot_{kind}{i}" if after is None else f"w_packed{after}_0"
                slots[i] = keep.tile([P, PAIR], dtype, name=f"slot_{kind}{i}", tag=tag, align_bytes=64)
                nc.vector.tensor_copy(slots[i][:], window[:].indirect(offsets))

        w_block = {}

        def prepare(strip):
            e, lo, hi = strip
            packed = keep.tile([P, hi - lo, PACK], BF16, name=f"w_packed{e}_{lo}", align_bytes=64)
            if e == 0:
                for half in (0, HALF):
                    nc.scalar.copy(words(packed, half, half + HALF), planes(w_raw[e, half], 0, HALF))
            else:
                split = hi - lo - ON_VECTOR.get((e, lo), 0)
                nc.scalar.copy(words(packed, 0, split), planes(w_raw[e, lo], 0, split))
                if split < hi - lo:
                    nc.vector.tensor_copy(words(packed, split, hi - lo), planes(w_raw[e, lo], split, hi - lo))

            def quantise():
                codes = keep.tile([P, hi - lo], U32, name=f"w_codes{e}_{lo}", align_bytes=64)
                scales = keep.tile([P, hi - lo], U8, name=f"w_scales{e}_{lo}", align_bytes=64)
                nc.vector.quantize_mx(
                    out=codes[:].bitcast(FP8X4), scales=scales[:], in_=packed[:].rearrange("p n t -> p (n t)")
                )
                for f in range(lo // P, hi // P):
                    w_block[e, f] = (codes, scales, slice(f * P - lo, (f + 1) * P - lo))

            return quantise

        y = [keep.tile([P, E * C], F32, name=f"y{f}") for f in range(BLOCKS)]
        activated = {}

        def multiply(i, f):
            acc = psum.tile([P, PAIR], F32, name="acc")
            for s in range(2):
                slots = slice(s * C, (s + 1) * C)
                codes, scales, features = w_block[2 * i + s, f]
                nc.tensor.matmul_mx(
                    out=acc[:, slots],
                    lhsT=codes[:, features].bitcast(FP8X4),
                    lhsT_scale=scales[:, features],
                    rhs=slot_codes[i][:, slots].bitcast(FP8X4),
                    rhs_scale=slot_scales[i][:, slots],
                    start=True,
                    stop=True,
                )
            first = i if f == 0 else 0
            last = i if f == 0 else PAIRS - 1
            width = (last - first + 1) * PAIR
            if i == first:
                activated[f] = work.tile([P, width], F32, name=f"activated{width}")
            r = activated[f]
            for s in range(2):
                e = 2 * i + s
                at = e * C - first * PAIR
                nc.scalar.activation(r[:, at : at + C], acc[:, s * C : (s + 1) * C], RELU, bias=bias[:, f, e : e + 1])
            if i == last:
                nc.scalar.activation(y[f][:, first * PAIR : first * PAIR + width], r[:], SQUARE)

        def fetch(f, r, lo, hi):
            part = work.tile([P, hi - lo], F32, name=f"part{r}_{lo}_{hi}")
            offsets = pos_lists[r][:, lo // OFFSETS_A_COLUMN : hi // OFFSETS_A_COLUMN]
            nc.vector.tensor_tensor(part[:], y[f][:].indirect(offsets), gates[f, r][:, lo:hi], MULT)
            return part

        def finish(f, parts, first, lo, hi):
            total = work.tile([P, hi - lo], F32, name=f"total_{lo}_{hi}")
            columns = slice(lo - first, hi - first)
            if (f, lo, hi) in SUMS_ON_TENSOR:
                bank = psum.tile([P, PAIR], F32, name="bank", bufs=2)
                for r in range(2):
                    nc.tensor.matmul(
                        bank[:, : hi - lo], identity[:], parts[r][:, columns], start=(r == 0), stop=(r == 1)
                    )
                nc.scalar.copy(total[:], bank[:, : hi - lo])
            else:
                nc.vector.tensor_tensor(total[:], parts[0][:, columns], parts[1][:, columns], ADD)
            nc.sync.dma_start(out[f * P : (f + 1) * P, lo:hi], total[:])

        gather(0)
        prepare(STRIPS[0])()
        prepare(STRIPS[1])()
        quantise = prepare(STRIPS[2])
        gather(1)
        multiply(0, 0)
        quantise()
        gather(2)
        prepare(STRIPS[3])()
        quantise = prepare(STRIPS[4])
        multiply(1, 0)
        quantise()
        prepare(STRIPS[5])()
        multiply(2, 0)
        for strip in STRIPS[6:]:
            prepare(strip)()

        parts0 = [fetch(0, r, 0, T) for r in range(2)]
        for f in (1, 2):
            for i in range(PAIRS):
                multiply(i, f)
        parts1 = [fetch(1, r, 0, T) for r in range(2)]
        for i in range(PAIRS):
            multiply(i, 3)
        finish(0, parts0, 0, 0, 512)
        finish(0, parts0, 0, 512, T)
        parts2 = [fetch(2, r, 0, T) for r in range(2)]
        finish(1, parts1, 0, 448, T)
        finish(1, parts1, 0, 0, 448)
        parts3 = [fetch(3, r, 0, LAST_CUT) for r in range(2)]
        finish(2, parts2, 0, 0, T)
        late = [fetch(3, 0, LAST_CUT, T)]
        finish(3, parts3, 0, 0, LAST_CUT)
        late.append(fetch(3, 1, LAST_CUT, T))
        finish(3, late, LAST_CUT, LAST_CUT, T)
